import numpy as np
import ml_dtypes


def mxq(x, axis, fmt="e4m3"):
    dtype, down = {"e4m3": (ml_dtypes.float8_e4m3fn, 7), "e5m2": (ml_dtypes.float8_e5m2, 14)}[fmt]
    v = np.moveaxis(np.asarray(x, np.float32).astype(ml_dtypes.bfloat16).astype(np.float64), axis, -1)
    blocks = v.reshape(v.shape[:-1] + (-1, 32))
    amax = np.abs(blocks).max(-1, keepdims=True)
    byte = np.maximum(np.where(amax > 0, np.frexp(amax)[1] - 1 + 127, 0) - down, 1)
    scale = np.exp2(byte - 127.0)
    codes = (blocks / scale).astype(np.float32).astype(dtype).astype(np.float64)
    return np.moveaxis((codes * scale).reshape(v.shape), -1, axis)


WIDE = False


def mx_kscale(k):
    if not WIDE:
        return np.ones(k)
    levels = np.array([10, -10, 5, -5, 0])
    if k % 512:
        return np.exp2(np.random.permutation(np.resize(levels, k // 32))).repeat(32)
    a = np.empty((k // 512, 16))
    for p in range(k // 512):
        a[p, :8] = np.random.permutation(np.resize(levels, 8))
        for g in range(8):
            far = levels[np.abs(levels - a[p, g]) >= 10]
            a[p, g + 8] = far[np.random.randint(len(far))]
    return np.exp2(a.ravel()).repeat(32)


def f64(x):
    return np.asarray(x).astype(np.float64)


def striped(idx):
    return np.tile(idx.reshape(-1, 16).T, (8, 1)).astype(np.uint16)


def unstriped(offs):
    return offs[:16].T.reshape(-1).astype(np.int64)


E2M1 = np.array([0.0, 0.5, 1.0, 1.5, 2.0, 3.0, 4.0, 6.0, -0.0, -0.5, -1.0, -1.5, -2.0, -3.0, -4.0, -6.0])


def pack_weight(w, fmt):
    k, n = w.shape
    w = f64(np.asarray(w, np.float32).astype(ml_dtypes.bfloat16)).reshape(k // 32, 32, n)
    amax = np.abs(w).max(1)
    if fmt == "e4m3":
        byte = np.frexp(amax)[1] - 1 + 127 - 7
    else:
        mant, ex = np.frexp(amax / 6.0)
        byte = np.where(mant > 0.5, ex, ex - 1) + 127
    byte = np.clip(np.where(amax > 0, byte, 1), 1, 254)
    scaled = (w * np.exp2(127.0 - byte)[:, None, :]).reshape(k, n).astype(np.float32)
    by_word = np.ascontiguousarray(scaled.reshape(k // 512, 128, 4, n).transpose(0, 1, 3, 2))
    if fmt == "e4m3":
        words = by_word.astype(ml_dtypes.float8_e4m3fn).view(np.uint8)
    else:
        c = by_word.astype(ml_dtypes.float4_e2m1fn).view(np.uint8) & 0xF
        words = (c[..., 0::2] | (c[..., 1::2] << 4)).reshape(k // 512, 128, 2 * n)
    return np.ascontiguousarray(words), np.ascontiguousarray(byte.astype(np.uint8).reshape(k // 512, 16, n))


def unpack_weight(words, scales, fmt):
    g, _, n = scales.shape
    words = np.ascontiguousarray(words).reshape(g, 128, n, -1)
    if fmt == "e4m3":
        vals = words.view(ml_dtypes.float8_e4m3fn).astype(np.float64)
    else:
        nib = np.empty((g, 128, n, 4), np.uint8)
        nib[..., 0::2] = words & 0xF
        nib[..., 1::2] = words >> 4
        vals = E2M1[nib]
    vals = vals * np.repeat(np.exp2(scales.astype(np.float64) - 127.0), 8, axis=1)[..., None]
    return vals.transpose(0, 1, 3, 2).reshape(g * 512, n)


def gelu(v):
    return 0.5 * v * (1.0 + np.tanh(np.sqrt(2.0 / np.pi) * (v + 0.044715 * v**3)))


K, KA, T, S, H, T3, S2, P = 1536, 512, 2048, 1024, 1024, 2048, 512, 512

def setup_inputs():
    n = np.random.standard_normal
    s = mx_kscale(K)[:, None]
    u = mx_kscale(H)[:, None]
    tab_words, tab_scales = pack_weight(n((K, T)) * s, "e4m3")
    tab2_words, tab2_scales = pack_weight(n((H, T3)) / np.sqrt(H) / u, "e4m3")
    w4_words, w4_scales = pack_weight(1.3 * n((K - KA, H)) / np.sqrt(K) / s[KA:], "e2m1")
    return {
        "tab_words": tab_words, "tab_scales": tab_scales,
        "offs": striped(np.random.permutation(T)[:S]),
        "tab2_words": tab2_words, "tab2_scales": tab2_scales,
        "offs2": striped(np.random.permutation(T3)[:S2]),
        "pos1": striped(np.random.permutation(S)[:P]),
        "pos2": striped(np.random.permutation(S)[:P]),
        "w1": (1.3 * n((KA, H)) / np.sqrt(K) / s[:KA]).astype(np.float32),
        "w4_words": w4_words, "w4_scales": w4_scales,
        "gm": n((H, S)).astype(np.float32),
        "gain": (1.3 * np.exp(0.3 * n(H)) * u[:, 0]).astype(np.float32),
        "am": (0.7 * n((H, P)) * u).astype(np.float32),
        "rota": (0.8 * n((S2, P))).astype(np.float32),
    }

def reference(tab_words, tab_scales, offs, tab2_words, tab2_scales, offs2, pos1, pos2,
              w1, w4_words, w4_scales, gm, gain, am, rota):
    v = unpack_weight(tab_words, tab_scales, "e4m3")[:, unstriped(offs)]
    v2 = unpack_weight(tab2_words, tab2_scales, "e4m3")[:, unstriped(offs2)]
    w1q = mxq(f64(w1), 0, "e4m3")
    w4 = unpack_weight(w4_words, w4_scales, "e2m1")
    y = w1q.T @ v[:KA] + w4.T @ v[KA:]
    h = f64(gain)[:, None] * (np.tanh(y) * f64(gm))
    x1 = mxq(h[:, unstriped(pos1)], 0, "e4m3")
    x2 = mxq(h[:, unstriped(pos2)] + f64(am), 0, "e4m3")
    e1 = v2.T @ x1
    e2 = v2.T @ x2
    return e1 * e2 + f64(rota)

@@ -1,0 +1,278 @@
+from contextlib import ExitStack
+
+import concourse.mybir as mybir
+
+K, KA, T, S, H, T3, S2, PICK = 1536, 512, 2048, 1024, 1024, 2048, 512, 512
+FLOPS = 2 * K * H * S + 2 * 2 * H * S2 * PICK
+
+F32 = mybir.dt.float32
+BF16 = mybir.dt.bfloat16
+I32 = mybir.dt.int32
+U32 = mybir.dt.uint32
+U16 = mybir.dt.uint16
+U8 = mybir.dt.uint8
+FP8X4 = mybir.dt.float8_e4m3fn_x4
+FP4X4 = mybir.dt.float4_e2m1fn_x4
+MULT = mybir.AluOpType.mult
+ADD = mybir.AluOpType.add
+ACT = mybir.ActivationFunctionType
+
+P = 128
+PACK = 4
+BLOCK = P * PACK
+BANK = 512
+QUADS = 4
+LIVE = 100
+TAB_ROW = 20
+VECTOR_TILES = 1
+GPSIMD_ADDS = 2
+
+
+def tile_list_instructor_slot_scores_kernel(
+    tc, tab_words, tab_scales, offs, tab2_words, tab2_scales, offs2, pos1, pos2,
+    w1, w4_words, w4_scales, gm, gain, am, rota, out,
+):
+    nc = tc.nc
+    blocks = H // BLOCK
+
+    with ExitStack() as ctx:
+        keep = ctx.enter_context(tc.tile_pool(name="keep", bufs=1))
+        ring = ctx.enter_context(tc.tile_pool(name="ring", bufs=2))
+        psum = ctx.enter_context(tc.psum_pool(name="psum", bufs=1))
+
+        def load_list(src, name):
+            tile = keep.tile(list(src.shape), U16, name=name)
+            nc.sync.dma_start(tile[:], src)
+            return tile
+
+        def load_scale_rows(queue, tile, src, first):
+            passes = src.shape[0]
+            for q in range(QUADS):
+                queue.dma_start(
+                    out=tile[32 * q + first : 32 * q + first + 4 * passes, :].bitcast(I32),
+                    in_=src[:, 4 * q : 4 * q + 4, :].bitcast(I32),
+                )
+
+        def load_words(src, name, tag):
+            tile = keep.tile([P, src.shape[1]], I32, name=name, tag=tag, align_bytes=64)
+            nc.sync.dma_start(out=tile[:], in_=src.rearrange("p n i -> p (n i)").bitcast(I32))
+            return tile
+
+        def lower_plane(dst, src, first):
+            nc.scalar.dma_start(out=dst[0:LIVE, :].bitcast(I32), in_=src[first : first + LIVE, :].bitcast(I32))
+
+        tab_s = keep.tile([P, T], U8, tag="scale_rows", align_bytes=64)
+        for q in range(QUADS):
+            nc.vector.memset(tab_s[32 * q : 32 * q + TAB_ROW, :].bitcast(I32), 0)
+        w4_s = keep.tile([P, 2, H], U8, align_bytes=64)
+        nc.gpsimd.memset(w4_s[:].bitcast(I32), 0)
+        v_s = {a: keep.tile([P, S], U8, name=f"v_s{a}", align_bytes=64) for a in (1, 2, 0)}
+        for tile in (v_s[1], v_s[2], v_s[0]):
+            nc.vector.memset(tile[96:P, :].bitcast(I32), 0)
+
+        offs_t = load_list(offs, "offs_t")
+        load_scale_rows(nc.sync, tab_s, tab_scales, TAB_ROW)
+        for q in range(QUADS):
+            nc.gpsimd.dma_start(
+                out=w4_s[32 * q : 32 * q + 4, :, :].bitcast(I32),
+                in_=w4_scales[:, 4 * q : 4 * q + 4, :].rearrange("a r c -> r a c").bitcast(I32),
+            )
+        tab_w = {a: load_words(tab_words[a], f"tab_w{a}", f"slot{a}") for a in (1, 2, 0)}
+        w4_w = keep.tile([P, 2, 2 * H], U8, align_bytes=64)
+        nc.sync.dma_start(out=w4_w[:].bitcast(I32), in_=w4_words.rearrange("a p c -> p a c").bitcast(I32))
+
+        w1_rows = w1.rearrange("(p j) c -> p j c", j=PACK)
+        gm_rows = gm.rearrange("(b p u t) c -> b u p t c", p=P, u=2, t=2)
+        am_rows = am.rearrange("(b p t) c -> b p t c", p=P, t=PACK)
+
+        def load_w1(b):
+            tile = keep.tile([P, PACK, BLOCK], F32, name=f"w1_raw{b}", tag="slot3", align_bytes=64)
+            nc.sync.dma_start(out=tile[:], in_=w1_rows[:, :, b * BLOCK : (b + 1) * BLOCK])
+            return tile
+
+        gm_t = {}
+
+        def load_gm(pair, tag):
+            tile = keep.tile([P, 2, S], F32, name=f"gm{pair}", tag=tag, align_bytes=64)
+            nc.sync.dma_start(out=tile[:], in_=gm_rows[pair // 2, pair % 2])
+            for t in range(2):
+                gm_t[2 * pair + t] = tile[:, t, :]
+
+        def load_am(b, tag):
+            tile = keep.tile([P, PACK, PICK], F32, name=f"am{b}", tag=tag, align_bytes=64)
+            nc.sync.dma_start(out=tile[:], in_=am_rows[b])
+            return tile
+
+        w1_raw = {0: load_w1(0)}
+        gain_t = keep.tile([P, blocks, PACK], F32)
+        nc.gpsimd.dma_start(out=gain_t[:], in_=gain.rearrange("(b p t) -> p b t", p=P, t=PACK))
+        pos1_t = load_list(pos1, "pos1_t")
+        pos2_t = load_list(pos2, "pos2_t")
+        offs2_t = load_list(offs2, "offs2_t")
+
+        v_s_packed = keep.tile([P, S], U8, align_bytes=64)
+        nc.vector.tensor_copy(v_s_packed[:], tab_s[:].indirect(offs_t[:]))
+        for a in (1, 2, 0):
+            lower_plane(v_s[a], v_s_packed, TAB_ROW + 4 * a)
+        tab2_s = keep.tile([P, T3], U8, tag="scale_rows", align_bytes=64)
+        nc.gpsimd.memset(tab2_s[:].bitcast(I32), 0)
+        load_scale_rows(nc.gpsimd, tab2_s, tab2_scales, 0)
+
+        v_w = {}
+        for a in (1, 2, 0):
+            v_w[a] = keep.tile([P, S], U32, name=f"v_w{a}", align_bytes=64)
+            nc.vector.tensor_copy(v_w[a][:], tab_w[a][:].bitcast(U32).indirect(offs_t[:]))
+
+        load_gm(0, "slot1")
+        tab2_w = {0: load_words(tab2_words[0], "tab2_w0", "slot2")}
+        load_gm(1, "slot0")
+
+        w4_dealt = {}
+        w4_plane = {}
+
+        def deal_w4(b):
+            cols = slice(b * BLOCK, (b + 1) * BLOCK)
+            w4_dealt[b] = keep.tile([P, 2, 2 * BLOCK], U8, name=f"w4_dealt{b}", align_bytes=64)
+            nc.scalar.copy(
+                out=w4_dealt[b][:].bitcast(U16).rearrange("p a (t m) -> p a m t", t=PACK),
+                in_=w4_w[:].bitcast(U16)[:, :, cols].rearrange("p a (m t) -> p a m t", t=PACK),
+            )
+            w4_plane[b] = keep.tile([P, 2, BLOCK], U8, name=f"w4_plane{b}", align_bytes=64)
+            nc.vector.tensor_copy(
+                out=w4_plane[b][:].rearrange("p a (t m) -> p a t m", t=PACK),
+                in_=w4_s[:, :, cols].rearrange("p a (m t) -> p a t m", t=PACK),
+            )
+
+        deal_w4(0)
+
+        w1_q = {}
+
+        def quantise_w1(engine_copy, b, t0, t1):
+            count = t1 - t0
+            grouped = keep.tile([P, count * BLOCK], BF16, name=f"w1_bf{b}_{t0}", align_bytes=64)
+            engine_copy(
+                out=grouped[:].rearrange("p (t m j) -> p m j t", t=count, j=PACK),
+                in_=w1_raw[b][:].rearrange("p j (m t) -> p m j t", t=PACK)[:, :, :, t0:t1],
+            )
+            codes = keep.tile([P, count * P], U32, name=f"w1_c{b}_{t0}", align_bytes=64)
+            plane = keep.tile([P, count * P], U8, name=f"w1_s{b}_{t0}", align_bytes=64)
+            nc.vector.quantize_mx(out=codes[:].bitcast(FP8X4), scales=plane[:], in_=grouped[:])
+            for t in range(t0, t1):
+                cols = slice((t - t0) * P, (t - t0 + 1) * P)
+                w1_q[b, t] = (codes[:, cols], plane[:, cols])
+
+        quantise_w1(nc.scalar.copy, 0, 0, 1)
+        quantise_w1(nc.vector.tensor_copy, 0, 1, PACK)
+        w1_raw[1] = load_w1(1)
+        am_t = {}
+
+        v2_w = {}
+        v2_s = keep.tile([P, S2], U8, align_bytes=64)
+
+        def gather_tab2(b):
+            v2_w[b] = keep.tile([P, S2], U32, name=f"v2_w{b}", align_bytes=64)
+            nc.vector.tensor_copy(v2_w[b][:], tab2_w[b][:].bitcast(U32).indirect(offs2_t[:]))
+
+        banks = 2 * (S2 // P)
+        e_acc = {}
+
+        def by_fours(ap_planes):
+            return ap_planes.rearrange("p t (c i) -> p c t i", i=PACK)
+
+        def woven(ap_flat):
+            return ap_flat.rearrange("p (c i t) -> p c t i", i=PACK, t=PACK)
+
+        x_q = {}
+        for b in range(blocks):
+            g1 = ring.tile([P, PACK, PICK], F32, name="g1")
+            g2 = keep.tile([P, PACK, PICK], F32, name="g2")
+            for t in range(PACK):
+                n = PACK * b + t
+                th = ring.tile([P, S], F32, name="th", bufs=4)
+                h = ring.tile([P, S], F32, name="h", bufs=3)
+                gain_col = gain_t[:, b, t : t + 1]
+                if n >= VECTOR_TILES:
+                    nc.scalar.activation(gm_t[n], gm_t[n], ACT.Copy, scale=gain_col)
+                for half in range(S // BANK):
+                    cols = slice(half * BANK, (half + 1) * BANK)
+                    acc = psum.tile([P, BANK], F32, name=f"y{n}_{half}", tag=f"bank{(2 * n + half) % banks}")
+                    for a in (1, 2):
+                        nc.tensor.matmul_mx(
+                            out=acc[:],
+                            lhsT=w4_dealt[b][:, a - 1, 2 * P * t : 2 * P * (t + 1)].bitcast(FP4X4),
+                            lhsT_scale=w4_plane[b][:, a - 1, P * t : P * (t + 1)],
+                            rhs=v_w[a][:, cols].bitcast(FP8X4),
+                            rhs_scale=v_s[a][:, cols],
+                            start=(a == 1), stop=False,
+                        )
+                    nc.tensor.matmul_mx(
+                        out=acc[:],
+                        lhsT=w1_q[b, t][0].bitcast(FP8X4),
+                        lhsT_scale=w1_q[b, t][1],
+                        rhs=v_w[0][:, cols].bitcast(FP8X4),
+                        rhs_scale=v_s[0][:, cols],
+                        start=False, stop=True,
+                    )
+                    nc.scalar.activation(th[:, cols], acc[:], ACT.Tanh)
+                    if n >= VECTOR_TILES:
+                        nc.gpsimd.tensor_tensor(h[:, cols], th[:, cols], gm_t[n][:, cols], MULT)
+                if n < VECTOR_TILES:
+                    nc.vector.scalar_tensor_tensor(h[:], th[:], gain_col, gm_t[n], MULT, MULT)
+                nc.vector.tensor_copy(g1[:, t, :], h[:].indirect(pos1_t[:]))
+                nc.vector.tensor_copy(g2[:, t, :], h[:].indirect(pos2_t[:]))
+                if n == 0:
+                    gather_tab2(0)
+                    nc.vector.tensor_copy(v2_s[:], tab2_s[:].indirect(offs2_t[:]))
+                    load_gm(2, "slot2")
+                if n == 1:
+                    deal_w4(1)
+                    quantise_w1(nc.scalar.copy, 1, 0, PACK)
+                    am_t[0] = load_am(0, "slot1")
+                    tab2_w[1] = load_words(tab2_words[1], "tab2_w1", "slot3")
+                if n == 3:
+                    load_gm(3, "slot0")
+                    gather_tab2(1)
+                    am_t[1] = load_am(1, "slot3")
+                if n == 5:
+                    rota_t = keep.tile([P, S2 // P, PICK], F32, tag="slot2", align_bytes=64)
+                    nc.sync.dma_start(out=rota_t[:], in_=rota.rearrange("(c p) j -> p c j", p=P))
+
+            x1_bf = keep.tile([P, PACK * PICK], BF16, name="x1_bf", align_bytes=64)
+            nc.scalar.copy(out=woven(x1_bf[:]), in_=by_fours(g1[:]))
+            x2_bf = keep.tile([P, PACK * PICK], BF16, name="x2_bf", align_bytes=64)
+            nc.vector.tensor_tensor(woven(x2_bf[:]), by_fours(g2[:]), by_fours(am_t[b][:]), ADD)
+            for which, x_bf in ((1, x1_bf), (2, x2_bf)):
+                codes = keep.tile([P, PICK], U32, name=f"x{which}_c{b}", align_bytes=64)
+                plane = keep.tile([P, PICK], U8, name=f"x{which}_s{b}", align_bytes=64)
+                nc.vector.quantize_mx(out=codes[:].bitcast(FP8X4), scales=plane[:], in_=x_bf[:])
+                x_q[which, b] = (codes, plane)
+
+        for which in (1, 2):
+            for c in range(S2 // P):
+                e_acc[which, c] = psum.tile(
+                    [P, PICK], F32, name=f"e{which}_{c}", tag=f"bank{(which - 1) * (S2 // P) + c}"
+                )
+        for b in range(blocks):
+            for which in (1, 2):
+                codes, plane = x_q[which, b]
+                for c in range(S2 // P):
+                    m_cols = slice(c * P, (c + 1) * P)
+                    nc.tensor.matmul_mx(
+                        out=e_acc[which, c][:],
+                        lhsT=v2_w[b][:, m_cols].bitcast(FP8X4),
+                        lhsT_scale=v2_s[4 * b :, m_cols],
+                        rhs=codes[:].bitcast(FP8X4),
+                        rhs_scale=plane[:],
+                        start=(b == 0), stop=(b == blocks - 1),
+                    )
+
+        e1_s = keep.tile([P, S2 // P, PICK], F32, align_bytes=64)
+        out_rows = out.rearrange("(c p) j -> c p j", p=P)
+        for c in range(S2 // P):
+            nc.scalar.copy(out=e1_s[:, c, :], in_=e_acc[1, c][:])
+        for c in range(S2 // P):
+            nc.vector.tensor_tensor(e1_s[:, c, :], e_acc[2, c][:], e1_s[:, c, :], MULT)
+        for c in range(S2 // P):
+            adder = nc.gpsimd if c < GPSIMD_ADDS else nc.vector
+            adder.tensor_tensor(rota_t[:, c, :], e1_s[:, c, :], rota_t[:, c, :], ADD)
+            nc.sync.dma_start(out=out_rows[c], in_=rota_t[:, c, :])

@@ -2,7 +2,7 @@ from contextlib import ExitStack
 
 import concourse.mybir as mybir
 
-K, KA, T, S, H, T3, S2, PICK = 1536, 512, 2048, 1024, 1024, 2048, 512, 512
+K, T, S, H, T3, S2, PICK = 1536, 2048, 1024, 1024, 2048, 512, 512
 FLOPS = 2 * K * H * S + 2 * 2 * H * S2 * PICK
 
 F32 = mybir.dt.float32
@@ -22,10 +22,14 @@ PACK = 4
 BLOCK = P * PACK
 BANK = 512
 QUADS = 4
-LIVE = 100
-TAB_ROW = 20
-VECTOR_TILES = 1
-GPSIMD_ADDS = 2
+QUAD = 32
+ROWS = 4
+LAST_QUAD = (QUADS - 1) * QUAD
+LIVE = LAST_QUAD + ROWS
+TAB_ROW = QUAD - 3 * ROWS
+VECTOR_TILES = 2
+GPSIMD_ADDS = 1
+AHEAD = 4
 
 
 def tile_list_instructor_slot_scores_kernel(
@@ -34,6 +38,9 @@ def tile_list_instructor_slot_scores_kernel(
 ):
     nc = tc.nc
     blocks = H // BLOCK
+    tiles = blocks * PACK
+    groups = S2 // P
+    banks = 2 * groups
 
     with ExitStack() as ctx:
         keep = ctx.enter_context(tc.tile_pool(name="keep", bufs=1))
@@ -45,12 +52,12 @@ def tile_list_instructor_slot_scores_kernel(
             nc.sync.dma_start(tile[:], src)
             return tile
 
-        def load_scale_rows(queue, tile, src, first):
+        def load_scale_rows(tile, src, first):
             passes = src.shape[0]
-            for q in range(QUADS):
-                queue.dma_start(
-                    out=tile[32 * q + first : 32 * q + first + 4 * passes, :].bitcast(I32),
-                    in_=src[:, 4 * q : 4 * q + 4, :].bitcast(I32),
+            for quad in range(QUADS):
+                nc.sync.dma_start(
+                    out=tile[QUAD * quad + first : QUAD * quad + first + ROWS * passes, :].bitcast(I32),
+                    in_=src[:, ROWS * quad : ROWS * (quad + 1), :].bitcast(I32),
                 )
 
         def load_words(src, name, tag):
@@ -59,34 +66,37 @@ def tile_list_instructor_slot_scores_kernel(
             return tile
 
         def lower_plane(dst, src, first):
-            nc.scalar.dma_start(out=dst[0:LIVE, :].bitcast(I32), in_=src[first : first + LIVE, :].bitcast(I32))
+            nc.sync.dma_start(out=dst[0:LIVE, :].bitcast(I32), in_=src[first : first + LIVE, :].bitcast(I32))
 
-        tab_s = keep.tile([P, T], U8, tag="scale_rows", align_bytes=64)
-        for q in range(QUADS):
-            nc.vector.memset(tab_s[32 * q : 32 * q + TAB_ROW, :].bitcast(I32), 0)
-        w4_s = keep.tile([P, 2, H], U8, align_bytes=64)
+        tab_s = keep.tile([P, T], U8, align_bytes=64)
+        for quad in range(QUADS):
+            nc.vector.memset(tab_s[QUAD * quad : QUAD * quad + TAB_ROW, :].bitcast(I32), 0)
+        w4_s = keep.tile([P, 2, H], U8, tag="scale_rows", align_bytes=64)
         nc.gpsimd.memset(w4_s[:].bitcast(I32), 0)
-        v_s = {a: keep.tile([P, S], U8, name=f"v_s{a}", align_bytes=64) for a in (1, 2, 0)}
-        for tile in (v_s[1], v_s[2], v_s[0]):
-            nc.vector.memset(tile[96:P, :].bitcast(I32), 0)
+        pass_order = (1, 2, 0)
+        v_s = {a: keep.tile([P, S], U8, name=f"v_s{a}", align_bytes=64) for a in pass_order}
+        for a in pass_order:
+            nc.vector.memset(v_s[a][LAST_QUAD:P, :].bitcast(I32), 0)
 
         offs_t = load_list(offs, "offs_t")
-        load_scale_rows(nc.sync, tab_s, tab_scales, TAB_ROW)
-        for q in range(QUADS):
+        load_scale_rows(tab_s, tab_scales, TAB_ROW)
+        for quad in range(QUADS):
             nc.gpsimd.dma_start(
-                out=w4_s[32 * q : 32 * q + 4, :, :].bitcast(I32),
-                in_=w4_scales[:, 4 * q : 4 * q + 4, :].rearrange("a r c -> r a c").bitcast(I32),
+                out=w4_s[QUAD * quad : QUAD * quad + ROWS, :, :].bitcast(I32),
+                in_=w4_scales[:, ROWS * quad : ROWS * (quad + 1), :].rearrange("a r c -> r a c").bitcast(I32),
             )
-        tab_w = {a: load_words(tab_words[a], f"tab_w{a}", f"slot{a}") for a in (1, 2, 0)}
+        tab_w = {1: load_words(tab_words[1], "tab_w1", "slot1")}
         w4_w = keep.tile([P, 2, 2 * H], U8, align_bytes=64)
         nc.sync.dma_start(out=w4_w[:].bitcast(I32), in_=w4_words.rearrange("a p c -> p a c").bitcast(I32))
+        for a in pass_order[1:]:
+            tab_w[a] = load_words(tab_words[a], f"tab_w{a}", f"slot{a}")
 
         w1_rows = w1.rearrange("(p j) c -> p j c", j=PACK)
-        gm_rows = gm.rearrange("(b p u t) c -> b u p t c", p=P, u=2, t=2)
+        gm_rows = gm.rearrange("(b p u e) c -> b u p e c", p=P, u=2, e=2)
         am_rows = am.rearrange("(b p t) c -> b p t c", p=P, t=PACK)
 
-        def load_w1(b):
-            tile = keep.tile([P, PACK, BLOCK], F32, name=f"w1_raw{b}", tag="slot3", align_bytes=64)
+        def load_w1(b, tag):
+            tile = keep.tile([P, PACK, BLOCK], F32, name=f"w1_raw{b}", tag=tag, align_bytes=64)
             nc.sync.dma_start(out=tile[:], in_=w1_rows[:, :, b * BLOCK : (b + 1) * BLOCK])
             return tile
 
@@ -95,15 +105,15 @@ def tile_list_instructor_slot_scores_kernel(
         def load_gm(pair, tag):
             tile = keep.tile([P, 2, S], F32, name=f"gm{pair}", tag=tag, align_bytes=64)
             nc.sync.dma_start(out=tile[:], in_=gm_rows[pair // 2, pair % 2])
-            for t in range(2):
-                gm_t[2 * pair + t] = tile[:, t, :]
+            for e in range(2):
+                gm_t[2 * pair + e] = tile[:, e, :]
 
         def load_am(b, tag):
             tile = keep.tile([P, PACK, PICK], F32, name=f"am{b}", tag=tag, align_bytes=64)
             nc.sync.dma_start(out=tile[:], in_=am_rows[b])
             return tile
 
-        w1_raw = {0: load_w1(0)}
+        w1_raw = {0: load_w1(0, "slot3")}
         gain_t = keep.tile([P, blocks, PACK], F32)
         nc.gpsimd.dma_start(out=gain_t[:], in_=gain.rearrange("(b p t) -> p b t", p=P, t=PACK))
         pos1_t = load_list(pos1, "pos1_t")
@@ -112,19 +122,16 @@ def tile_list_instructor_slot_scores_kernel(
 
         v_s_packed = keep.tile([P, S], U8, align_bytes=64)
         nc.vector.tensor_copy(v_s_packed[:], tab_s[:].indirect(offs_t[:]))
-        for a in (1, 2, 0):
-            lower_plane(v_s[a], v_s_packed, TAB_ROW + 4 * a)
-        tab2_s = keep.tile([P, T3], U8, tag="scale_rows", align_bytes=64)
-        nc.gpsimd.memset(tab2_s[:].bitcast(I32), 0)
-        load_scale_rows(nc.gpsimd, tab2_s, tab2_scales, 0)
+        for a in pass_order:
+            lower_plane(v_s[a], v_s_packed, TAB_ROW + ROWS * a)
 
         v_w = {}
-        for a in (1, 2, 0):
+        for a in pass_order:
             v_w[a] = keep.tile([P, S], U32, name=f"v_w{a}", align_bytes=64)
             nc.vector.tensor_copy(v_w[a][:], tab_w[a][:].bitcast(U32).indirect(offs_t[:]))
 
         load_gm(0, "slot1")
-        tab2_w = {0: load_words(tab2_words[0], "tab2_w0", "slot2")}
+        w1_raw[1] = load_w1(1, "slot2")
         load_gm(1, "slot0")
 
         w4_dealt = {}
@@ -132,24 +139,28 @@ def tile_list_instructor_slot_scores_kernel(
 
         def deal_w4(b):
             cols = slice(b * BLOCK, (b + 1) * BLOCK)
-            w4_dealt[b] = keep.tile([P, 2, 2 * BLOCK], U8, name=f"w4_dealt{b}", align_bytes=64)
+            w4_dealt[b] = keep.tile([P, 2, 2 * BLOCK], U8, name=f"w4_dealt{b}", tag=f"woven{1 - b}", align_bytes=64)
             nc.scalar.copy(
                 out=w4_dealt[b][:].bitcast(U16).rearrange("p a (t m) -> p a m t", t=PACK),
                 in_=w4_w[:].bitcast(U16)[:, :, cols].rearrange("p a (m t) -> p a m t", t=PACK),
             )
             w4_plane[b] = keep.tile([P, 2, BLOCK], U8, name=f"w4_plane{b}", align_bytes=64)
-            nc.vector.tensor_copy(
+            nc.gpsimd.tensor_copy(
                 out=w4_plane[b][:].rearrange("p a (t m) -> p a t m", t=PACK),
                 in_=w4_s[:, :, cols].rearrange("p a (m t) -> p a t m", t=PACK),
             )
 
-        deal_w4(0)
+        for b in range(blocks):
+            deal_w4(b)
+        tab2_s = keep.tile([P, T3], U8, tag="scale_rows", align_bytes=64)
+        nc.gpsimd.memset(tab2_s[:].bitcast(I32), 0)
+        load_scale_rows(tab2_s, tab2_scales, 0)
 
         w1_q = {}
 
         def quantise_w1(engine_copy, b, t0, t1):
             count = t1 - t0
-            grouped = keep.tile([P, count * BLOCK], BF16, name=f"w1_bf{b}_{t0}", align_bytes=64)
+            grouped = keep.tile([P, count * BLOCK], BF16, name=f"w1_bf{b}_{t0}", tag=f"w1_bf{b}_{t0}", align_bytes=64)
             engine_copy(
                 out=grouped[:].rearrange("p (t m j) -> p m j t", t=count, j=PACK),
                 in_=w1_raw[b][:].rearrange("p j (m t) -> p m j t", t=PACK)[:, :, :, t0:t1],
@@ -163,8 +174,9 @@ def tile_list_instructor_slot_scores_kernel(
 
         quantise_w1(nc.scalar.copy, 0, 0, 1)
         quantise_w1(nc.vector.tensor_copy, 0, 1, PACK)
-        w1_raw[1] = load_w1(1)
-        am_t = {}
+        load_gm(2, "slot3")
+        am_t = {0: load_am(0, "w1_bf0_1")}
+        tab2_w = {}
 
         v2_w = {}
         v2_s = keep.tile([P, S2], U8, align_bytes=64)
@@ -173,30 +185,50 @@ def tile_list_instructor_slot_scores_kernel(
             v2_w[b] = keep.tile([P, S2], U32, name=f"v2_w{b}", align_bytes=64)
             nc.vector.tensor_copy(v2_w[b][:], tab2_w[b][:].bitcast(U32).indirect(offs2_t[:]))
 
-        banks = 2 * (S2 // P)
-        e_acc = {}
-
-        def by_fours(ap_planes):
-            return ap_planes.rearrange("p t (c i) -> p c t i", i=PACK)
+        def by_fours(ap_tiles):
+            return ap_tiles.rearrange("p t (c i) -> p c t i", i=PACK)
 
         def woven(ap_flat):
             return ap_flat.rearrange("p (c i t) -> p c t i", i=PACK, t=PACK)
 
         x_q = {}
+        picked = {}
+        width = PACK * PICK
+
+        def quantise_block(b):
+            g1, g2 = picked[b]
+            x_bf = keep.tile([P, 2, width], BF16, name=f"x_bf{b}", tag=f"woven{b}", align_bytes=64)
+            nc.scalar.copy(out=woven(x_bf[:, 0, :]), in_=by_fours(g1[:]))
+            nc.vector.tensor_tensor(woven(x_bf[:, 1, :]), by_fours(g2[:]), by_fours(am_t[b][:]), ADD)
+            codes = keep.tile([P, 2, PICK], U32, name=f"x_c{b}", align_bytes=64)
+            plane = keep.tile([P, 2, PICK], U8, name=f"x_s{b}", align_bytes=64)
+            if b < blocks - 1:
+                nc.vector.quantize_mx(
+                    out=codes[:].rearrange("p w j -> p (w j)").bitcast(FP8X4),
+                    scales=plane[:].rearrange("p w j -> p (w j)"),
+                    in_=x_bf[:].rearrange("p w j -> p (w j)"),
+                )
+            else:
+                for w in range(2):
+                    nc.vector.quantize_mx(out=codes[:, w, :].bitcast(FP8X4), scales=plane[:, w, :], in_=x_bf[:, w, :])
+            for w in range(2):
+                x_q[w + 1, b] = (codes[:, w, :], plane[:, w, :])
+
         for b in range(blocks):
             g1 = ring.tile([P, PACK, PICK], F32, name="g1")
-            g2 = keep.tile([P, PACK, PICK], F32, name="g2")
+            g2 = ring.tile([P, PACK, PICK], F32, name="g2")
+            picked[b] = (g1, g2)
             for t in range(PACK):
                 n = PACK * b + t
-                th = ring.tile([P, S], F32, name="th", bufs=4)
-                h = ring.tile([P, S], F32, name="h", bufs=3)
+                th = ring.tile([P, S], F32, name="th", bufs=AHEAD)
+                h = ring.tile([P, S], F32, name="h", bufs=AHEAD)
                 gain_col = gain_t[:, b, t : t + 1]
                 if n >= VECTOR_TILES:
                     nc.scalar.activation(gm_t[n], gm_t[n], ACT.Copy, scale=gain_col)
                 for half in range(S // BANK):
                     cols = slice(half * BANK, (half + 1) * BANK)
                     acc = psum.tile([P, BANK], F32, name=f"y{n}_{half}", tag=f"bank{(2 * n + half) % banks}")
-                    for a in (1, 2):
+                    for a in pass_order[:2]:
                         nc.tensor.matmul_mx(
                             out=acc[:],
                             lhsT=w4_dealt[b][:, a - 1, 2 * P * t : 2 * P * (t + 1)].bitcast(FP4X4),
@@ -218,61 +250,54 @@ def tile_list_instructor_slot_scores_kernel(
                         nc.gpsimd.tensor_tensor(h[:, cols], th[:, cols], gm_t[n][:, cols], MULT)
                 if n < VECTOR_TILES:
                     nc.vector.scalar_tensor_tensor(h[:], th[:], gain_col, gm_t[n], MULT, MULT)
+                if n == tiles - 1:
+                    quantise_block(0)
                 nc.vector.tensor_copy(g1[:, t, :], h[:].indirect(pos1_t[:]))
                 nc.vector.tensor_copy(g2[:, t, :], h[:].indirect(pos2_t[:]))
-                if n == 0:
+                if n == 1:
+                    load_gm(3, "slot1")
+                if n == 3:
+                    quantise_w1(nc.scalar.copy, 1, 0, PACK)
+                    tab2_w[0] = load_words(tab2_words[0], "tab2_w0", "slot2")
                     gather_tab2(0)
                     nc.vector.tensor_copy(v2_s[:], tab2_s[:].indirect(offs2_t[:]))
-                    load_gm(2, "slot2")
-                if n == 1:
-                    deal_w4(1)
-                    quantise_w1(nc.scalar.copy, 1, 0, PACK)
-                    am_t[0] = load_am(0, "slot1")
-                    tab2_w[1] = load_words(tab2_words[1], "tab2_w1", "slot3")
-                if n == 3:
-                    load_gm(3, "slot0")
+                    tab2_w[1] = load_words(tab2_words[1], "tab2_w1", "slot0")
                     gather_tab2(1)
-                    am_t[1] = load_am(1, "slot3")
                 if n == 5:
-                    rota_t = keep.tile([P, S2 // P, PICK], F32, tag="slot2", align_bytes=64)
+                    am_t[1] = load_am(1, "slot3")
+                if n == 7:
+                    rota_t = keep.tile([P, groups, PICK], F32, tag="slot1", align_bytes=64)
                     nc.sync.dma_start(out=rota_t[:], in_=rota.rearrange("(c p) j -> p c j", p=P))
 
-            x1_bf = keep.tile([P, PACK * PICK], BF16, name="x1_bf", align_bytes=64)
-            nc.scalar.copy(out=woven(x1_bf[:]), in_=by_fours(g1[:]))
-            x2_bf = keep.tile([P, PACK * PICK], BF16, name="x2_bf", align_bytes=64)
-            nc.vector.tensor_tensor(woven(x2_bf[:]), by_fours(g2[:]), by_fours(am_t[b][:]), ADD)
-            for which, x_bf in ((1, x1_bf), (2, x2_bf)):
-                codes = keep.tile([P, PICK], U32, name=f"x{which}_c{b}", align_bytes=64)
-                plane = keep.tile([P, PICK], U8, name=f"x{which}_s{b}", align_bytes=64)
-                nc.vector.quantize_mx(out=codes[:].bitcast(FP8X4), scales=plane[:], in_=x_bf[:])
-                x_q[which, b] = (codes, plane)
+        quantise_block(1)
 
+        e_acc = {}
         for which in (1, 2):
-            for c in range(S2 // P):
+            for c in range(groups):
                 e_acc[which, c] = psum.tile(
-                    [P, PICK], F32, name=f"e{which}_{c}", tag=f"bank{(which - 1) * (S2 // P) + c}"
+                    [P, PICK], F32, name=f"e{which}_{c}", tag=f"bank{(which - 1) * groups + c}"
                 )
         for b in range(blocks):
-            for which in (1, 2):
-                codes, plane = x_q[which, b]
-                for c in range(S2 // P):
+            for c in range(groups):
+                for which in (1, 2):
+                    codes, plane = x_q[which, b]
                     m_cols = slice(c * P, (c + 1) * P)
                     nc.tensor.matmul_mx(
                         out=e_acc[which, c][:],
                         lhsT=v2_w[b][:, m_cols].bitcast(FP8X4),
-                        lhsT_scale=v2_s[4 * b :, m_cols],
-                        rhs=codes[:].bitcast(FP8X4),
-                        rhs_scale=plane[:],
+                        lhsT_scale=v2_s[ROWS * b :, m_cols],
+                        rhs=codes.bitcast(FP8X4),
+                        rhs_scale=plane,
                         start=(b == 0), stop=(b == blocks - 1),
                     )
 
-        e1_s = keep.tile([P, S2 // P, PICK], F32, align_bytes=64)
+        e1_s = keep.tile([P, groups, PICK], F32, align_bytes=64)
         out_rows = out.rearrange("(c p) j -> c p j", p=P)
-        for c in range(S2 // P):
+        for c in range(groups):
             nc.scalar.copy(out=e1_s[:, c, :], in_=e_acc[1, c][:])
-        for c in range(S2 // P):
+        for c in range(groups):
             nc.vector.tensor_tensor(e1_s[:, c, :], e_acc[2, c][:], e1_s[:, c, :], MULT)
-        for c in range(S2 // P):
+        for c in range(groups):
             adder = nc.gpsimd if c < GPSIMD_ADDS else nc.vector
             adder.tensor_tensor(rota_t[:, c, :], e1_s[:, c, :], rota_t[:, c, :], ADD)
             nc.sync.dma_start(out=out_rows[c], in_=rota_t[:, c, :])

from contextlib import ExitStack

import concourse.mybir as mybir

K, T, S, H, T3, S2, PICK = 1536, 2048, 1024, 1024, 2048, 512, 512
FLOPS = 2 * K * H * S + 2 * 2 * H * S2 * PICK

F32 = mybir.dt.float32
BF16 = mybir.dt.bfloat16
I32 = mybir.dt.int32
U32 = mybir.dt.uint32
U16 = mybir.dt.uint16
U8 = mybir.dt.uint8
FP8X4 = mybir.dt.float8_e4m3fn_x4
FP4X4 = mybir.dt.float4_e2m1fn_x4
MULT = mybir.AluOpType.mult
ADD = mybir.AluOpType.add
ACT = mybir.ActivationFunctionType

P = 128
PACK = 4
BLOCK = P * PACK
BANK = 512
QUADS = 4
QUAD = 32
ROWS = 4
LAST_QUAD = (QUADS - 1) * QUAD
LIVE = LAST_QUAD + ROWS
TAB_ROW = QUAD - 3 * ROWS
VECTOR_TILES = 2
GPSIMD_ADDS = 1
AHEAD = 4


def tile_list_instructor_slot_scores_kernel(
    tc, tab_words, tab_scales, offs, tab2_words, tab2_scales, offs2, pos1, pos2,
    w1, w4_words, w4_scales, gm, gain, am, rota, out,
):
    nc = tc.nc
    blocks = H // BLOCK
    tiles = blocks * PACK
    groups = S2 // P
    banks = 2 * groups

    with ExitStack() as ctx:
        keep = ctx.enter_context(tc.tile_pool(name="keep", bufs=1))
        ring = ctx.enter_context(tc.tile_pool(name="ring", bufs=2))
        psum = ctx.enter_context(tc.psum_pool(name="psum", bufs=1))

        def load_list(src, name):
            tile = keep.tile(list(src.shape), U16, name=name)
            nc.sync.dma_start(tile[:], src)
            return tile

        def load_scale_rows(tile, src, first):
            passes = src.shape[0]
            for quad in range(QUADS):
                nc.sync.dma_start(
                    out=tile[QUAD * quad + first : QUAD * quad + first + ROWS * passes, :].bitcast(I32),
                    in_=src[:, ROWS * quad : ROWS * (quad + 1), :].bitcast(I32),
                )

        def load_words(src, name, tag):
            tile = keep.tile([P, src.shape[1]], I32, name=name, tag=tag, align_bytes=64)
            nc.sync.dma_start(out=tile[:], in_=src.rearrange("p n i -> p (n i)").bitcast(I32))
            return tile

        def lower_plane(dst, src, first):
            nc.sync.dma_start(out=dst[0:LIVE, :].bitcast(I32), in_=src[first : first + LIVE, :].bitcast(I32))

        tab_s = keep.tile([P, T], U8, align_bytes=64)
        for quad in range(QUADS):
            nc.vector.memset(tab_s[QUAD * quad : QUAD * quad + TAB_ROW, :].bitcast(I32), 0)
        w4_s = keep.tile([P, 2, H], U8, tag="scale_rows", align_bytes=64)
        nc.gpsimd.memset(w4_s[:].bitcast(I32), 0)
        pass_order = (1, 2, 0)
        v_s = {a: keep.tile([P, S], U8, name=f"v_s{a}", align_bytes=64) for a in pass_order}
        for a in pass_order:
            nc.vector.memset(v_s[a][LAST_QUAD:P, :].bitcast(I32), 0)

        offs_t = load_list(offs, "offs_t")
        load_scale_rows(tab_s, tab_scales, TAB_ROW)
        for quad in range(QUADS):
            nc.gpsimd.dma_start(
                out=w4_s[QUAD * quad : QUAD * quad + ROWS, :, :].bitcast(I32),
                in_=w4_scales[:, ROWS * quad : ROWS * (quad + 1), :].rearrange("a r c -> r a c").bitcast(I32),
            )
        tab_w = {1: load_words(tab_words[1], "tab_w1", "slot1")}
        w4_w = keep.tile([P, 2, 2 * H], U8, align_bytes=64)
        nc.sync.dma_start(out=w4_w[:].bitcast(I32), in_=w4_words.rearrange("a p c -> p a c").bitcast(I32))
        for a in pass_order[1:]:
            tab_w[a] = load_words(tab_words[a], f"tab_w{a}", f"slot{a}")

        w1_rows = w1.rearrange("(p j) c -> p j c", j=PACK)
        gm_rows = gm.rearrange("(b p u e) c -> b u p e c", p=P, u=2, e=2)
        am_rows = am.rearrange("(b p t) c -> b p t c", p=P, t=PACK)

        def load_w1(b, tag):
            tile = keep.tile([P, PACK, BLOCK], F32, name=f"w1_raw{b}", tag=tag, align_bytes=64)
            nc.sync.dma_start(out=tile[:], in_=w1_rows[:, :, b * BLOCK : (b + 1) * BLOCK])
            return tile

        gm_t = {}

        def load_gm(pair, tag):
            tile = keep.tile([P, 2, S], F32, name=f"gm{pair}", tag=tag, align_bytes=64)
            nc.sync.dma_start(out=tile[:], in_=gm_rows[pair // 2, pair % 2])
            for e in range(2):
                gm_t[2 * pair + e] = tile[:, e, :]

        def load_am(b, tag):
            tile = keep.tile([P, PACK, PICK], F32, name=f"am{b}", tag=tag, align_bytes=64)
            nc.sync.dma_start(out=tile[:], in_=am_rows[b])
            return tile

        w1_raw = {0: load_w1(0, "slot3")}
        gain_t = keep.tile([P, blocks, PACK], F32)
        nc.gpsimd.dma_start(out=gain_t[:], in_=gain.rearrange("(b p t) -> p b t", p=P, t=PACK))
        pos1_t = load_list(pos1, "pos1_t")
        pos2_t = load_list(pos2, "pos2_t")
        offs2_t = load_list(offs2, "offs2_t")

        v_s_packed = keep.tile([P, S], U8, align_bytes=64)
        nc.vector.tensor_copy(v_s_packed[:], tab_s[:].indirect(offs_t[:]))
        for a in pass_order:
            lower_plane(v_s[a], v_s_packed, TAB_ROW + ROWS * a)

        v_w = {}
        for a in pass_order:
            v_w[a] = keep.tile([P, S], U32, name=f"v_w{a}", align_bytes=64)
            nc.vector.tensor_copy(v_w[a][:], tab_w[a][:].bitcast(U32).indirect(offs_t[:]))

        load_gm(0, "slot1")
        w1_raw[1] = load_w1(1, "slot2")
        load_gm(1, "slot0")

        w4_dealt = {}
        w4_plane = {}

        def deal_w4(b):
            cols = slice(b * BLOCK, (b + 1) * BLOCK)
            w4_dealt[b] = keep.tile([P, 2, 2 * BLOCK], U8, name=f"w4_dealt{b}", tag=f"woven{1 - b}", align_bytes=64)
            nc.scalar.copy(
                out=w4_dealt[b][:].bitcast(U16).rearrange("p a (t m) -> p a m t", t=PACK),
                in_=w4_w[:].bitcast(U16)[:, :, cols].rearrange("p a (m t) -> p a m t", t=PACK),
            )
            w4_plane[b] = keep.tile([P, 2, BLOCK], U8, name=f"w4_plane{b}", align_bytes=64)
            nc.gpsimd.tensor_copy(
                out=w4_plane[b][:].rearrange("p a (t m) -> p a t m", t=PACK),
                in_=w4_s[:, :, cols].rearrange("p a (m t) -> p a t m", t=PACK),
            )

        for b in range(blocks):
            deal_w4(b)
        tab2_s = keep.tile([P, T3], U8, tag="scale_rows", align_bytes=64)
        nc.gpsimd.memset(tab2_s[:].bitcast(I32), 0)
        load_scale_rows(tab2_s, tab2_scales, 0)

        w1_q = {}

        def quantise_w1(engine_copy, b, t0, t1):
            count = t1 - t0
            grouped = keep.tile([P, count * BLOCK], BF16, name=f"w1_bf{b}_{t0}", tag=f"w1_bf{b}_{t0}", align_bytes=64)
            engine_copy(
                out=grouped[:].rearrange("p (t m j) -> p m j t", t=count, j=PACK),
                in_=w1_raw[b][:].rearrange("p j (m t) -> p m j t", t=PACK)[:, :, :, t0:t1],
            )
            codes = keep.tile([P, count * P], U32, name=f"w1_c{b}_{t0}", align_bytes=64)
            plane = keep.tile([P, count * P], U8, name=f"w1_s{b}_{t0}", align_bytes=64)
            nc.vector.quantize_mx(out=codes[:].bitcast(FP8X4), scales=plane[:], in_=grouped[:])
            for t in range(t0, t1):
                cols = slice((t - t0) * P, (t - t0 + 1) * P)
                w1_q[b, t] = (codes[:, cols], plane[:, cols])

        quantise_w1(nc.scalar.copy, 0, 0, 1)
        quantise_w1(nc.vector.tensor_copy, 0, 1, PACK)
        load_gm(2, "slot3")
        am_t = {0: load_am(0, "w1_bf0_1")}
        tab2_w = {}

        v2_w = {}
        v2_s = keep.tile([P, S2], U8, align_bytes=64)

        def gather_tab2(b):
            v2_w[b] = keep.tile([P, S2], U32, name=f"v2_w{b}", align_bytes=64)
            nc.vector.tensor_copy(v2_w[b][:], tab2_w[b][:].bitcast(U32).indirect(offs2_t[:]))

        def by_fours(ap_tiles):
            return ap_tiles.rearrange("p t (c i) -> p c t i", i=PACK)

        def woven(ap_flat):
            return ap_flat.rearrange("p (c i t) -> p c t i", i=PACK, t=PACK)

        x_q = {}
        picked = {}
        width = PACK * PICK

        def quantise_block(b):
            g1, g2 = picked[b]
            x_bf = keep.tile([P, 2, width], BF16, name=f"x_bf{b}", tag=f"woven{b}", align_bytes=64)
            nc.scalar.copy(out=woven(x_bf[:, 0, :]), in_=by_fours(g1[:]))
            nc.vector.tensor_tensor(woven(x_bf[:, 1, :]), by_fours(g2[:]), by_fours(am_t[b][:]), ADD)
            codes = keep.tile([P, 2, PICK], U32, name=f"x_c{b}", align_bytes=64)
            plane = keep.tile([P, 2, PICK], U8, name=f"x_s{b}", align_bytes=64)
            if b < blocks - 1:
                nc.vector.quantize_mx(
                    out=codes[:].rearrange("p w j -> p (w j)").bitcast(FP8X4),
                    scales=plane[:].rearrange("p w j -> p (w j)"),
                    in_=x_bf[:].rearrange("p w j -> p (w j)"),
                )
            else:
                for w in range(2):
                    nc.vector.quantize_mx(out=codes[:, w, :].bitcast(FP8X4), scales=plane[:, w, :], in_=x_bf[:, w, :])
            for w in range(2):
                x_q[w + 1, b] = (codes[:, w, :], plane[:, w, :])

        for b in range(blocks):
            g1 = ring.tile([P, PACK, PICK], F32, name="g1")
            g2 = ring.tile([P, PACK, PICK], F32, name="g2")
            picked[b] = (g1, g2)
            for t in range(PACK):
                n = PACK * b + t
                th = ring.tile([P, S], F32, name="th", bufs=AHEAD)
                h = ring.tile([P, S], F32, name="h", bufs=AHEAD)
                gain_col = gain_t[:, b, t : t + 1]
                if n >= VECTOR_TILES:
                    nc.scalar.activation(gm_t[n], gm_t[n], ACT.Copy, scale=gain_col)
                for half in range(S // BANK):
                    cols = slice(half * BANK, (half + 1) * BANK)
                    acc = psum.tile([P, BANK], F32, name=f"y{n}_{half}", tag=f"bank{(2 * n + half) % banks}")
                    for a in pass_order[:2]:
                        nc.tensor.matmul_mx(
                            out=acc[:],
                            lhsT=w4_dealt[b][:, a - 1, 2 * P * t : 2 * P * (t + 1)].bitcast(FP4X4),
                            lhsT_scale=w4_plane[b][:, a - 1, P * t : P * (t + 1)],
                            rhs=v_w[a][:, cols].bitcast(FP8X4),
                            rhs_scale=v_s[a][:, cols],
                            start=(a == 1), stop=False,
                        )
                    nc.tensor.matmul_mx(
                        out=acc[:],
                        lhsT=w1_q[b, t][0].bitcast(FP8X4),
                        lhsT_scale=w1_q[b, t][1],
                        rhs=v_w[0][:, cols].bitcast(FP8X4),
                        rhs_scale=v_s[0][:, cols],
                        start=False, stop=True,
                    )
                    nc.scalar.activation(th[:, cols], acc[:], ACT.Tanh)
                    if n >= VECTOR_TILES:
                        nc.gpsimd.tensor_tensor(h[:, cols], th[:, cols], gm_t[n][:, cols], MULT)
                if n < VECTOR_TILES:
                    nc.vector.scalar_tensor_tensor(h[:], th[:], gain_col, gm_t[n], MULT, MULT)
                if n == tiles - 1:
                    quantise_block(0)
                nc.vector.tensor_copy(g1[:, t, :], h[:].indirect(pos1_t[:]))
                nc.vector.tensor_copy(g2[:, t, :], h[:].indirect(pos2_t[:]))
                if n == 1:
                    load_gm(3, "slot1")
                if n == 3:
                    quantise_w1(nc.scalar.copy, 1, 0, PACK)
                    tab2_w[0] = load_words(tab2_words[0], "tab2_w0", "slot2")
                    gather_tab2(0)
                    nc.vector.tensor_copy(v2_s[:], tab2_s[:].indirect(offs2_t[:]))
                    tab2_w[1] = load_words(tab2_words[1], "tab2_w1", "slot0")
                    gather_tab2(1)
                if n == 5:
                    am_t[1] = load_am(1, "slot3")
                if n == 7:
                    rota_t = keep.tile([P, groups, PICK], F32, tag="slot1", align_bytes=64)
                    nc.sync.dma_start(out=rota_t[:], in_=rota.rearrange("(c p) j -> p c j", p=P))

        quantise_block(1)

        e_acc = {}
        for which in (1, 2):
            for c in range(groups):
                e_acc[which, c] = psum.tile(
                    [P, PICK], F32, name=f"e{which}_{c}", tag=f"bank{(which - 1) * groups + c}"
                )
        for b in range(blocks):
            for c in range(groups):
                for which in (1, 2):
                    codes, plane = x_q[which, b]
                    m_cols = slice(c * P, (c + 1) * P)
                    nc.tensor.matmul_mx(
                        out=e_acc[which, c][:],
                        lhsT=v2_w[b][:, m_cols].bitcast(FP8X4),
                        lhsT_scale=v2_s[ROWS * b :, m_cols],
                        rhs=codes.bitcast(FP8X4),
                        rhs_scale=plane,
                        start=(b == 0), stop=(b == blocks - 1),
                    )

        e1_s = keep.tile([P, groups, PICK], F32, align_bytes=64)
        out_rows = out.rearrange("(c p) j -> c p j", p=P)
        for c in range(groups):
            nc.scalar.copy(out=e1_s[:, c, :], in_=e_acc[1, c][:])
        for c in range(groups):
            nc.vector.tensor_tensor(e1_s[:, c, :], e_acc[2, c][:], e1_s[:, c, :], MULT)
        for c in range(groups):
            adder = nc.gpsimd if c < GPSIMD_ADDS else nc.vector
            adder.tensor_tensor(rota_t[:, c, :], e1_s[:, c, :], rota_t[:, c, :], ADD)
            nc.sync.dma_start(out=out_rows[c], in_=rota_t[:, c, :])
